import numpy as np
import ml_dtypes

BF16 = ml_dtypes.bfloat16


def bf(x):
    return np.asarray(x, np.float32).astype(BF16)


def f32(x):
    return np.asarray(x, np.float32)


def f64(x):
    return np.asarray(x).astype(np.float64)


def striped(idx):
    return np.tile(idx.reshape(-1, 16).T, (8, 1))


S, K, M, N, D, V = 1024, 128, 256, 2048, 2, 1024


def setup_inputs():
    return {"table": bf(np.random.standard_normal((K, S))), "w": bf(np.random.standard_normal((K, M)) / np.sqrt(D * K)), "b": f32(0.5 * np.random.standard_normal((M, 1))), "offs": striped(np.random.permutation(np.tile(np.arange(S), 2))[:N])}


def reference(table, w, b, offs):
    idx = offs[:16].T.reshape(-1)
    x = f64(table)[:, idx]
    y = f64(w).T @ sum(x[:, t * V : (t + 1) * V] for t in range(D))
    return y + f64(b)

@@ -1,0 +1,47 @@
+import concourse.mybir as mybir
+
+BF16, F32, U16 = mybir.dt.bfloat16, mybir.dt.float32, mybir.dt.uint16
+ADD = mybir.AluOpType.add
+
+P = 128
+NODES = 1024
+OUT_FEATURES = 256
+NEIGHBOURS = 2
+BANK = 512
+PER_COLUMN = 16
+
+FLOPS = 2 * P * OUT_FEATURES * NEIGHBOURS * NODES
+
+
+def tile_gather_matmul_kernel(tc, table, w, b, offs, out):
+    nc = tc.nc
+    with (
+        tc.tile_pool(name="held", bufs=1) as held,
+        tc.tile_pool(name="staged", bufs=4) as staged,
+        tc.psum_pool(name="psum", bufs=4) as psum,
+    ):
+        offsets = held.tile([P, NEIGHBOURS * NODES // PER_COLUMN], U16, name="offsets")
+        nc.sync.dma_start(offsets[:], offs)
+        nodes = held.tile([P, NODES], BF16, name="nodes")
+        nc.scalar.dma_start(nodes[:], table)
+        weights = held.tile([P, OUT_FEATURES], BF16, name="weights")
+        nc.sync.dma_start(weights[:], w)
+        bias = held.tile([P, OUT_FEATURES // P], F32, name="bias")
+        with nc.allow_non_contiguous_dma(reason="256 single float32 values, one to a partition"):
+            nc.scalar.dma_start(bias[:], b.rearrange("(a p) o -> p (a o)", p=P))
+
+        for a in range(OUT_FEATURES // P):
+            for c in range(NODES // BANK):
+                bank = psum.tile([P, BANK], F32, name="bank")
+                for t in range(NEIGHBOURS):
+                    first = (t * NODES + c * BANK) // PER_COLUMN
+                    nc.tensor.matmul(
+                        bank[:],
+                        weights[:, a * P : (a + 1) * P],
+                        nodes[:].indirect(offsets[:, first : first + BANK // PER_COLUMN]),
+                        start=(t == 0),
+                        stop=(t == NEIGHBOURS - 1),
+                    )
+                result = staged.tile([P, BANK], F32, name="result")
+                nc.vector.tensor_scalar(result[:], bank[:], bias[:, a : a + 1], None, ADD)
+                nc.sync.dma_start(out[a * P : (a + 1) * P, c * BANK : (c + 1) * BANK], result[:])

@@ -32,16 +32,21 @@ def tile_gather_matmul_kernel(tc, table, w, b, offs, out):
 
         for a in range(OUT_FEATURES // P):
             for c in range(NODES // BANK):
-                bank = psum.tile([P, BANK], F32, name="bank")
-                for t in range(NEIGHBOURS):
-                    first = (t * NODES + c * BANK) // PER_COLUMN
-                    nc.tensor.matmul(
-                        bank[:],
-                        weights[:, a * P : (a + 1) * P],
-                        nodes[:].indirect(offsets[:, first : first + BANK // PER_COLUMN]),
-                        start=(t == 0),
-                        stop=(t == NEIGHBOURS - 1),
-                    )
+                is_last = a == OUT_FEATURES // P - 1 and c == NODES // BANK - 1
+                width = BANK // 2 if is_last else BANK
                 result = staged.tile([P, BANK], F32, name="result")
-                nc.vector.tensor_scalar(result[:], bank[:], bias[:, a : a + 1], None, ADD)
+                for left in range(0, BANK, width):
+                    bank = psum.tile([P, BANK], F32, name="bank")
+                    for t in range(NEIGHBOURS):
+                        first = (t * NODES + c * BANK + left) // PER_COLUMN
+                        nc.tensor.matmul(
+                            bank[:, :width],
+                            weights[:, a * P : (a + 1) * P],
+                            nodes[:].indirect(offsets[:, first : first + width // PER_COLUMN]),
+                            start=(t == 0),
+                            stop=(t == NEIGHBOURS - 1),
+                        )
+                    nc.vector.tensor_scalar(
+                        result[:, left : left + width], bank[:, :width], bias[:, a : a + 1], None, ADD
+                    )
                 nc.sync.dma_start(out[a * P : (a + 1) * P, c * BANK : (c + 1) * BANK], result[:])

@@ -9,6 +9,7 @@ OUT_FEATURES = 256
 NEIGHBOURS = 2
 BANK = 512
 PER_COLUMN = 16
+LAST_WIDTHS = (256, 128, 128)
 
 FLOPS = 2 * P * OUT_FEATURES * NEIGHBOURS * NODES
 
@@ -33,9 +34,10 @@ def tile_gather_matmul_kernel(tc, table, w, b, offs, out):
         for a in range(OUT_FEATURES // P):
             for c in range(NODES // BANK):
                 is_last = a == OUT_FEATURES // P - 1 and c == NODES // BANK - 1
-                width = BANK // 2 if is_last else BANK
+                widths = LAST_WIDTHS if is_last else (BANK,)
                 result = staged.tile([P, BANK], F32, name="result")
-                for left in range(0, BANK, width):
+                left = 0
+                for width in widths:
                     bank = psum.tile([P, BANK], F32, name="bank")
                     for t in range(NEIGHBOURS):
                         first = (t * NODES + c * BANK + left) // PER_COLUMN
@@ -49,4 +51,5 @@ def tile_gather_matmul_kernel(tc, table, w, b, offs, out):
                     nc.vector.tensor_scalar(
                         result[:, left : left + width], bank[:, :width], bias[:, a : a + 1], None, ADD
                     )
+                    left += width
                 nc.sync.dma_start(out[a * P : (a + 1) * P, c * BANK : (c + 1) * BANK], result[:])

@@ -6,10 +6,13 @@ ADD = mybir.AluOpType.add
 P = 128
 NODES = 1024
 OUT_FEATURES = 256
+BLOCKS = OUT_FEATURES // P
 NEIGHBOURS = 2
 BANK = 512
+BANKS = 8
 PER_COLUMN = 16
-LAST_WIDTHS = (256, 128, 128)
+PLAIN_STORES = ((BANK,), (BANK,))
+LAST_STORES = ((384, 128, 128), (256, 128))
 
 FLOPS = 2 * P * OUT_FEATURES * NEIGHBOURS * NODES
 
@@ -18,8 +21,8 @@ def tile_gather_matmul_kernel(tc, table, w, b, offs, out):
     nc = tc.nc
     with (
         tc.tile_pool(name="held", bufs=1) as held,
-        tc.tile_pool(name="staged", bufs=4) as staged,
-        tc.psum_pool(name="psum", bufs=4) as psum,
+        tc.tile_pool(name="staged", bufs=2) as staged,
+        tc.psum_pool(name="psum", bufs=BANKS) as psum,
     ):
         offsets = held.tile([P, NEIGHBOURS * NODES // PER_COLUMN], U16, name="offsets")
         nc.sync.dma_start(offsets[:], offs)
@@ -27,20 +30,19 @@ def tile_gather_matmul_kernel(tc, table, w, b, offs, out):
         nc.scalar.dma_start(nodes[:], table)
         weights = held.tile([P, OUT_FEATURES], BF16, name="weights")
         nc.sync.dma_start(weights[:], w)
-        bias = held.tile([P, OUT_FEATURES // P], F32, name="bias")
+        bias = held.tile([P, BLOCKS], F32, name="bias")
         with nc.allow_non_contiguous_dma(reason="256 single float32 values, one to a partition"):
             nc.scalar.dma_start(bias[:], b.rearrange("(a p) o -> p (a o)", p=P))
 
-        for a in range(OUT_FEATURES // P):
-            for c in range(NODES // BANK):
-                is_last = a == OUT_FEATURES // P - 1 and c == NODES // BANK - 1
-                widths = LAST_WIDTHS if is_last else (BANK,)
-                result = staged.tile([P, BANK], F32, name="result")
-                left = 0
+        for a in range(BLOCKS):
+            result = staged.tile([P, NODES], F32, name="result")
+            left = 0
+            for widths in LAST_STORES if a == BLOCKS - 1 else PLAIN_STORES:
+                stored = left
                 for width in widths:
                     bank = psum.tile([P, BANK], F32, name="bank")
                     for t in range(NEIGHBOURS):
-                        first = (t * NODES + c * BANK + left) // PER_COLUMN
+                        first = (t * NODES + left) // PER_COLUMN
                         nc.tensor.matmul(
                             bank[:, :width],
                             weights[:, a * P : (a + 1) * P],
@@ -52,4 +54,4 @@ def tile_gather_matmul_kernel(tc, table, w, b, offs, out):
                         result[:, left : left + width], bank[:, :width], bias[:, a : a + 1], None, ADD
                     )
                     left += width
-                nc.sync.dma_start(out[a * P : (a + 1) * P, c * BANK : (c + 1) * BANK], result[:])
+                nc.sync.dma_start(out[a * P : (a + 1) * P, stored:left], result[:, stored:left])

@@ -11,6 +11,7 @@ NEIGHBOURS = 2
 BANK = 512
 BANKS = 8
 PER_COLUMN = 16
+DMA_ALIGN = 256
 PLAIN_STORES = ((BANK,), (BANK,))
 LAST_STORES = ((384, 128, 128), (256, 128))
 
@@ -24,18 +25,18 @@ def tile_gather_matmul_kernel(tc, table, w, b, offs, out):
         tc.tile_pool(name="staged", bufs=2) as staged,
         tc.psum_pool(name="psum", bufs=BANKS) as psum,
     ):
-        offsets = held.tile([P, NEIGHBOURS * NODES // PER_COLUMN], U16, name="offsets")
+        offsets = held.tile([P, NEIGHBOURS * NODES // PER_COLUMN], U16, name="offsets", align_bytes=DMA_ALIGN)
         nc.sync.dma_start(offsets[:], offs)
-        nodes = held.tile([P, NODES], BF16, name="nodes")
+        nodes = held.tile([P, NODES], BF16, name="nodes", align_bytes=DMA_ALIGN)
         nc.scalar.dma_start(nodes[:], table)
-        weights = held.tile([P, OUT_FEATURES], BF16, name="weights")
+        weights = held.tile([P, OUT_FEATURES], BF16, name="weights", align_bytes=DMA_ALIGN)
         nc.sync.dma_start(weights[:], w)
         bias = held.tile([P, BLOCKS], F32, name="bias")
         with nc.allow_non_contiguous_dma(reason="256 single float32 values, one to a partition"):
             nc.scalar.dma_start(bias[:], b.rearrange("(a p) o -> p (a o)", p=P))
 
         for a in range(BLOCKS):
-            result = staged.tile([P, NODES], F32, name="result")
+            result = staged.tile([P, NODES], F32, name="result", align_bytes=DMA_ALIGN)
             left = 0
             for widths in LAST_STORES if a == BLOCKS - 1 else PLAIN_STORES:
                 stored = left

@@ -11,7 +11,7 @@ NEIGHBOURS = 2
 BANK = 512
 BANKS = 8
 PER_COLUMN = 16
-DMA_ALIGN = 256
+DMA_ALIGN = 4096
 PLAIN_STORES = ((BANK,), (BANK,))
 LAST_STORES = ((384, 128, 128), (256, 128))
 

import concourse.mybir as mybir

BF16, F32, U16 = mybir.dt.bfloat16, mybir.dt.float32, mybir.dt.uint16
ADD = mybir.AluOpType.add

P = 128
NODES = 1024
OUT_FEATURES = 256
BLOCKS = OUT_FEATURES // P
NEIGHBOURS = 2
BANK = 512
BANKS = 8
PER_COLUMN = 16
DMA_ALIGN = 4096
PLAIN_STORES = ((BANK,), (BANK,))
LAST_STORES = ((384, 128, 128), (256, 128))

FLOPS = 2 * P * OUT_FEATURES * NEIGHBOURS * NODES


def tile_gather_matmul_kernel(tc, table, w, b, offs, out):
    nc = tc.nc
    with (
        tc.tile_pool(name="held", bufs=1) as held,
        tc.tile_pool(name="staged", bufs=2) as staged,
        tc.psum_pool(name="psum", bufs=BANKS) as psum,
    ):
        offsets = held.tile([P, NEIGHBOURS * NODES // PER_COLUMN], U16, name="offsets", align_bytes=DMA_ALIGN)
        nc.sync.dma_start(offsets[:], offs)
        nodes = held.tile([P, NODES], BF16, name="nodes", align_bytes=DMA_ALIGN)
        nc.scalar.dma_start(nodes[:], table)
        weights = held.tile([P, OUT_FEATURES], BF16, name="weights", align_bytes=DMA_ALIGN)
        nc.sync.dma_start(weights[:], w)
        bias = held.tile([P, BLOCKS], F32, name="bias")
        with nc.allow_non_contiguous_dma(reason="256 single float32 values, one to a partition"):
            nc.scalar.dma_start(bias[:], b.rearrange("(a p) o -> p (a o)", p=P))

        for a in range(BLOCKS):
            result = staged.tile([P, NODES], F32, name="result", align_bytes=DMA_ALIGN)
            left = 0
            for widths in LAST_STORES if a == BLOCKS - 1 else PLAIN_STORES:
                stored = left
                for width in widths:
                    bank = psum.tile([P, BANK], F32, name="bank")
                    for t in range(NEIGHBOURS):
                        first = (t * NODES + left) // PER_COLUMN
                        nc.tensor.matmul(
                            bank[:, :width],
                            weights[:, a * P : (a + 1) * P],
                            nodes[:].indirect(offsets[:, first : first + width // PER_COLUMN]),
                            start=(t == 0),
                            stop=(t == NEIGHBOURS - 1),
                        )
                    nc.vector.tensor_scalar(
                        result[:, left : left + width], bank[:, :width], bias[:, a : a + 1], None, ADD
                    )
                    left += width
                nc.sync.dma_start(out[a * P : (a + 1) * P, stored:left], result[:, stored:left])
